import numpy as np
import ml_dtypes


def mxq(x, axis, fmt="e4m3"):
    dtype, down = {"e4m3": (ml_dtypes.float8_e4m3fn, 7), "e5m2": (ml_dtypes.float8_e5m2, 14)}[fmt]
    v = np.moveaxis(np.asarray(x, np.float32).astype(ml_dtypes.bfloat16).astype(np.float64), axis, -1)
    blocks = v.reshape(v.shape[:-1] + (-1, 32))
    amax = np.abs(blocks).max(-1, keepdims=True)
    byte = np.maximum(np.where(amax > 0, np.frexp(amax)[1] - 1 + 127, 0) - down, 1)
    scale = np.exp2(byte - 127.0)
    codes = (blocks / scale).astype(np.float32).astype(dtype).astype(np.float64)
    return np.moveaxis((codes * scale).reshape(v.shape), -1, axis)


WIDE = False


def mx_kscale(k):
    if not WIDE:
        return np.ones(k)
    levels = np.array([10, -10, 5, -5, 0])
    if k % 512:
        return np.exp2(np.random.permutation(np.resize(levels, k // 32))).repeat(32)
    a = np.empty((k // 512, 16))
    for p in range(k // 512):
        a[p, :8] = np.random.permutation(np.resize(levels, 8))
        for g in range(8):
            far = levels[np.abs(levels - a[p, g]) >= 10]
            a[p, g + 8] = far[np.random.randint(len(far))]
    return np.exp2(a.ravel()).repeat(32)


BF16 = ml_dtypes.bfloat16


def bf(x):
    return np.asarray(x, np.float32).astype(BF16)


def f64(x):
    return np.asarray(x).astype(np.float64)


E2M1 = np.array([0.0, 0.5, 1.0, 1.5, 2.0, 3.0, 4.0, 6.0, -0.0, -0.5, -1.0, -1.5, -2.0, -3.0, -4.0, -6.0])


def pack_weight(w, fmt):
    k, n = w.shape
    w = f64(bf(w)).reshape(k // 32, 32, n)
    amax = np.abs(w).max(1)
    if fmt == "e4m3":
        byte = np.frexp(amax)[1] - 1 + 127 - 7
    else:
        mant, ex = np.frexp(amax / 6.0)
        byte = np.where(mant > 0.5, ex, ex - 1) + 127
    byte = np.clip(np.where(amax > 0, byte, 1), 1, 254)
    scaled = (w * np.exp2(127.0 - byte)[:, None, :]).reshape(k, n).astype(np.float32)
    by_word = np.ascontiguousarray(scaled.reshape(k // 512, 128, 4, n).transpose(0, 1, 3, 2))
    if fmt == "e4m3":
        words = by_word.astype(ml_dtypes.float8_e4m3fn).view(np.uint8)
    else:
        c = by_word.astype(ml_dtypes.float4_e2m1fn).view(np.uint8) & 0xF
        words = c[..., 0::2] | (c[..., 1::2] << 4)
    return np.ascontiguousarray(words), np.ascontiguousarray(byte.astype(np.uint8).reshape(k // 512, 16, n))


def unpack_weight(words, scales, fmt):
    g, p, n, _ = words.shape
    if fmt == "e4m3":
        vals = np.ascontiguousarray(words).view(ml_dtypes.float8_e4m3fn).astype(np.float64)
    else:
        nib = np.empty((g, p, n, 4), np.uint8)
        nib[..., 0::2] = words & 0xF
        nib[..., 1::2] = words >> 4
        vals = E2M1[nib]
    vals = vals * np.repeat(np.exp2(scales.astype(np.float64) - 127.0), 8, axis=1)[..., None]
    return vals.transpose(0, 1, 3, 2).reshape(g * 512, n)
def pack4(w):
    words, scales = pack_weight(w, "e2m1")
    return words.reshape(words.shape[0], 128, -1), scales


def unpack4(words, scales):
    return unpack_weight(words.reshape(words.shape[0], 128, -1, 2), scales, "e2m1")


def planes(Y):
    n, m = Y.shape
    b = f64(bf(Y)).reshape(n // 32, 32, m)
    amax = np.abs(b).max(1)
    byte = np.clip(np.where(amax > 0, np.frexp(amax)[1] - 1 + 127 - 7, 1), 1, 254)
    codes = (b * np.exp2(127.0 - byte)[:, None, :]).reshape(n, m).astype(np.float32).astype(ml_dtypes.float8_e4m3fn).view(np.uint8)
    words = codes.reshape(n // 512, 128, 4, m).transpose(0, 1, 3, 2)
    return np.ascontiguousarray(words), np.ascontiguousarray(byte.astype(np.uint8).reshape(n // 512, 16, m))


T, D, F, R = 2048, 1024, 1024, 512


def setup_inputs():
    s, t = mx_kscale(F), mx_kscale(T)
    x = bf(np.random.standard_normal((T, D)) / t[:, None])
    g = bf(np.random.standard_normal((T, F)) * s[None, :] * t[:, None])
    p = bf(np.random.standard_normal((D, R)))
    lam = bf(np.random.uniform(0.5, 1.5, R))
    q = np.random.standard_normal((R, F)) / np.sqrt(F) / s[None, :]
    q_words, q_scales = pack4(q.T)
    return {
        "x": x,
        "g": g,
        "p": p,
        "lam": lam,
        "q_words": q_words,
        "q_scales": q_scales,
        "avg_i": bf(np.random.uniform(0.2, 1.2, (D, R))),
        "avg_u": bf(np.random.uniform(0.2, 1.2, (D, R))),
    }


def factor_grad(x, g, lam, qt):
    u = mxq(g, 1, "e4m3") @ qt
    ul = u * lam[None, :]
    return (mxq(x, 0, "e4m3").T @ mxq(ul, 0, "e4m3")) / np.sqrt(T)


def core(x, g, p, lam, q_words, q_scales, avg_i, avg_u):
    grad = factor_grad(f64(x), f64(g), f64(lam), unpack4(q_words, q_scales))
    s = np.abs(f64(p) * grad)
    i_new = 0.7 * f64(avg_i) + 0.3 * s
    u_new = 0.7 * f64(avg_u) + 0.3 * np.abs(s - i_new)
    return i_new * u_new


def reference(x, g, p, lam, q_words, q_scales, avg_i, avg_u):
    R_out = core(x, g, p, lam, q_words, q_scales, avg_i, avg_u)
    words, scales = planes(R_out.T)
    return R_out, words, scales

@@ -1,0 +1,334 @@
+from contextlib import ExitStack
+import math
+
+import concourse.mybir as mybir
+from concourse.masks import make_identity
+
+T, D, F, R = 2048, 1024, 1024, 512
+FLOPS = 2 * T * F * R + 2 * T * D * R
+
+F32 = mybir.dt.float32
+BF16 = mybir.dt.bfloat16
+I32 = mybir.dt.int32
+U32 = mybir.dt.uint32
+U8 = mybir.dt.uint8
+E4M3 = mybir.dt.float8_e4m3fn_x4
+E2M1 = mybir.dt.float4_e2m1fn_x4
+ALU = mybir.AluOpType
+ACT = mybir.ActivationFunctionType
+
+P = 128
+NC = T // 512
+NB = D // P
+
+
+def tile_adalorasensitivityscore_x2_kernel(
+    tc, x, g, p, lam, q_words, q_scales, avg_i, avg_u, out_0, out_1, out_2
+):
+    nc = tc.nc
+    with ExitStack() as ctx:
+        keep = ctx.enter_context(tc.tile_pool(name="keep", bufs=1))
+        work = ctx.enter_context(tc.tile_pool(name="work", bufs=3))
+        ptr = ctx.enter_context(tc.psum_pool(name="ptr", bufs=4))
+        pacc = ctx.enter_context(tc.psum_pool(name="pacc", bufs=4))
+        ctx.enter_context(tc.manual_schedule())
+
+        g_sb = [keep.tile([P, 4, F], BF16, name="g%d" % c) for c in range(NC)]
+        x_sb = [[keep.tile([P, 4, 512], BF16, name="x%d_%d" % (c, h)) for h in range(2)] for c in range(NC)]
+        w_words = keep.tile([P, 2, 2 * R], U8, name="w_words", align_bytes=64)
+        w_scales = keep.tile([P, 2, R], U8, name="w_scales", align_bytes=64)
+        g_codes = [keep.tile([P, 1024], U32, name="gc%d" % c, align_bytes=64) for c in range(NC)]
+        g_scales = [keep.tile([P, 1024], U8, name="gs%d" % c, align_bytes=64) for c in range(NC)]
+        u_codes = [keep.tile([P, R], U32, name="uc%d" % c, align_bytes=64) for c in range(NC)]
+        u_scales = [keep.tile([P, R], U8, name="us%d" % c, align_bytes=64) for c in range(NC)]
+        x_codes = [keep.tile([P, D], U32, name="xc%d" % c, align_bytes=64) for c in range(NC)]
+        x_scales = [keep.tile([P, D], U8, name="xs%d" % c, align_bytes=64) for c in range(NC)]
+        o_codes = keep.tile([P, D], U32, name="o_codes", align_bytes=64)
+        o_scales = keep.tile([P, D], U8, name="o_scales", align_bytes=64)
+        p_sb = [keep.tile([P, 4, R], BF16, name="p%d" % h) for h in range(2)]
+        a_sb = [keep.tile([P, 4, R], BF16, name="a%d" % h) for h in range(2)]
+        b_sb = [keep.tile([P, 4, R], BF16, name="b%d" % h) for h in range(2)]
+        ident = keep.tile([P, P], F32, name="ident")
+        ident16 = keep.tile([P, P], BF16, name="ident16")
+        lam_sb = keep.tile([P, 4], BF16, name="lam_sb")
+        lam_bc = keep.tile([P, R], BF16, name="lam_bc")
+        warm = keep.tile([P, 1], F32, name="warm")
+
+        nc.vector.memset(w_scales[:].bitcast(I32), 0)
+        nc.vector.memset(warm[:], 1.0)
+        make_identity(nc, ident[:])
+        make_identity(nc, ident16[:])
+
+        def load_g(c, t0, t1):
+            nc.sync.dma_start(
+                out=g_sb[c][:, t0:t1, :],
+                in_=g[512 * c : 512 * (c + 1), :].rearrange("(p t) f -> p t f", t=4)[:, t0:t1, :],
+            )
+
+        def load_x(c, h):
+            nc.sync.dma_start(
+                out=x_sb[c][h][:],
+                in_=x[512 * c : 512 * (c + 1), 512 * h : 512 * (h + 1)].rearrange("(p t) f -> p t f", t=4),
+            )
+
+        def load_e(dst, src, h):
+            nc.sync.dma_start(
+                out=dst[h][:], in_=src[512 * h : 512 * (h + 1), :].rearrange("(i p) r -> p i r", p=P)
+            )
+
+        for t in range(4):
+            load_g(0, t, t + 1)
+        nc.sync.dma_start(
+            out=w_words[:].bitcast(I32), in_=q_words.rearrange("g p n -> p g n").bitcast(I32)
+        )
+        nc.scalar.dma_start(out=lam_sb[:], in_=lam.rearrange("(p m) -> p m", m=4))
+        for q in range(4):
+            nc.scalar.dma_start(
+                out=w_scales[32 * q : 32 * q + 4, :, :].bitcast(I32),
+                in_=q_scales[:, 4 * q : 4 * q + 4, :].rearrange("g q n -> q g n").bitcast(I32),
+            )
+        load_g(1, 0, 2)
+        load_g(1, 2, 4)
+        load_x(0, 0)
+        load_g(2, 0, 4)
+        load_x(1, 0)
+        load_g(3, 0, 4)
+        load_x(2, 0)
+        load_x(3, 0)
+        load_e(p_sb, p, 0)
+        load_e(a_sb, avg_i, 0)
+        load_e(b_sb, avg_u, 0)
+        for c in range(NC):
+            load_x(c, 1)
+        load_e(p_sb, p, 1)
+        load_e(a_sb, avg_i, 1)
+        load_e(b_sb, avg_u, 1)
+
+        nc.scalar.activation(out=warm[:], in_=warm[:], func=ACT.Abs)
+
+        gi = {}
+
+        def transposes(c):
+            for t in range(4):
+                if t % 2 == 0:
+                    gi[c, t // 2] = work.tile([P, 2048], BF16, name="gi", tag="gi", align_bytes=64)
+                bank = ptr.tile([P, 2, 2, P], F32, name="tr", tag="tr")
+                words = g_sb[c][:, t, :].bitcast(F32)
+                for k in range(2):
+                    for u in range(2):
+                        nc.tensor.transpose(
+                            bank[:, k, u, :], words[:, 256 * k + u : 256 * (k + 1) : 2], ident[:]
+                        )
+                dst = gi[c, t // 2][:].bitcast(F32)[:, 512 * (t % 2) : 512 * (t % 2 + 1)]
+                nc.scalar.copy(
+                    out=dst.rearrange("p (k r u) -> p k r u", k=2, u=2),
+                    in_=bank[:].rearrange("p k u r -> p k r u"),
+                )
+
+        def quant_g(c):
+            for h in range(2):
+                nc.vector.quantize_mx(
+                    out=g_codes[c][:, 512 * h : 512 * (h + 1)].bitcast(E4M3),
+                    scales=g_scales[c][:, 512 * h : 512 * (h + 1)],
+                    in_=gi[c, h][:],
+                )
+
+        acc = {}
+
+        def stage1(c):
+            for rb in range(4):
+                bank = pacc.tile([P, 512], F32, name="acc", tag="acc")
+                acc[c, rb] = bank
+                for t in range(4):
+                    for k in range(2):
+                        cols = slice((2 * t + k) * P, (2 * t + k + 1) * P)
+                        nc.tensor.matmul_mx(
+                            out=bank[:, P * t : P * (t + 1)],
+                            lhsT=g_codes[c][:, cols].bitcast(E4M3),
+                            lhsT_scale=g_scales[c][:, cols],
+                            rhs=w_words[:, k, 256 * rb : 256 * (rb + 1)].bitcast(E2M1),
+                            rhs_scale=w_scales[:, k, P * rb : P * (rb + 1)],
+                            start=(k == 0),
+                            stop=(k == 1),
+                        )
+
+        ui = {}
+
+        def times_lam(c):
+            ui[c] = work.tile([P, R, 4], BF16, name="ui", tag="ui", bufs=2, align_bytes=64)
+            for rb in range(4):
+                rs = slice(P * rb, P * (rb + 1))
+                nc.vector.tensor_tensor(
+                    out=ui[c][:, rs, :],
+                    in0=acc[c, rb][:].rearrange("p (t n) -> p n t", t=4),
+                    in1=lam_bc[:, rs].unsqueeze(2).to_broadcast([P, P, 4]),
+                    op=ALU.mult,
+                )
+
+        def quant_u(c):
+            nc.vector.quantize_mx(
+                out=u_codes[c][:].bitcast(E4M3), scales=u_scales[c][:], in_=ui[c][:].rearrange("p n t -> p (n t)")
+            )
+
+        xi = {}
+
+        def inter_x(c, col, width):
+            h, o = col // 512, col % 512
+            t = work.tile([P, width, 4], BF16, name="xi%d" % width, tag="xi%d" % width, align_bytes=64)
+            xi[c, col] = t
+            for s in range(0, width, 256):
+                nc.scalar.copy(
+                    out=t[:, s : s + 256, :],
+                    in_=x_sb[c][h][:, :, o + s : o + s + 256].rearrange("p t d -> p d t"),
+                )
+
+        def quant_x(c, col, width):
+            nc.vector.quantize_mx(
+                out=x_codes[c][:, col : col + width].bitcast(E4M3),
+                scales=x_scales[c][:, col : col + width],
+                in_=xi[c, col][:].rearrange("p d t -> p (d t)"),
+            )
+
+        transposes(0)
+        lbank = pacc.tile([P, 4, P], BF16, name="lbank", tag="acc")
+        for m in range(4):
+            nc.tensor.transpose(lbank[:, m, :], lam_sb[:, m : m + 1].to_broadcast([P, P]), ident16[:])
+        nc.scalar.copy(
+            out=lam_bc[:].rearrange("p (n m) -> p n m", m=4), in_=lbank[:].rearrange("p m n -> p n m")
+        )
+        quant_g(0)
+        transposes(1)
+        quant_g(1)
+        stage1(0)
+        inter_x(0, 0, 512)
+        times_lam(0)
+        transposes(2)
+        quant_x(0, 0, 512)
+        quant_u(0)
+        quant_g(2)
+        stage1(1)
+        inter_x(1, 0, 512)
+        times_lam(1)
+        transposes(3)
+        quant_x(1, 0, 512)
+        quant_u(1)
+        quant_g(3)
+        stage1(2)
+        inter_x(2, 0, 512)
+        times_lam(2)
+        stage1(3)
+        inter_x(3, 0, 512)
+        quant_x(2, 0, 512)
+        quant_u(2)
+        times_lam(3)
+        quant_x(3, 0, 512)
+        quant_u(3)
+
+        gacc, s_t, d_t, a_t, b_t, o_t, oi = {}, {}, {}, {}, {}, {}, {}
+
+        def stage2(i):
+            bank = pacc.tile([P, 512], F32, name="acc2", tag="acc")
+            gacc[i] = bank
+            cols = slice(P * i, P * (i + 1))
+            for c in range(NC):
+                nc.tensor.matmul_mx(
+                    out=bank[:],
+                    lhsT=x_codes[c][:, cols].bitcast(E4M3),
+                    lhsT_scale=x_scales[c][:, cols],
+                    rhs=u_codes[c][:].bitcast(E4M3),
+                    rhs_scale=u_scales[c][:],
+                    start=(c == 0),
+                    stop=(c == NC - 1),
+                )
+
+        def prod(i):
+            s_t[i] = work.tile([P, R], F32, name="s_t", tag="s_t")
+            nc.vector.tensor_tensor(out=s_t[i][:], in0=gacc[i][:], in1=p_sb[i // 4][:, i % 4, :], op=ALU.mult)
+
+        def abs_s(i):
+            nc.scalar.activation(out=s_t[i][:], in_=s_t[i][:], func=ACT.Abs, scale=1.0 / math.sqrt(T))
+
+        def diff(i):
+            d_t[i] = work.tile([P, R], F32, name="d_t", tag="d_t")
+            nc.vector.tensor_tensor(out=d_t[i][:], in0=s_t[i][:], in1=a_sb[i // 4][:, i % 4, :], op=ALU.subtract)
+
+        def abs_d(i):
+            nc.scalar.activation(out=d_t[i][:], in_=d_t[i][:], func=ACT.Abs, scale=0.21)
+
+        def i_new(i):
+            a_t[i] = work.tile([P, R], F32, name="a_t", tag="a_t")
+            nc.vector.scalar_tensor_tensor(
+                out=a_t[i][:], in0=s_t[i][:], scalar=0.3 / 0.7, in1=a_sb[i // 4][:, i % 4, :], op0=ALU.mult, op1=ALU.add
+            )
+
+        def u_new(i):
+            b_t[i] = work.tile([P, R], F32, name="b_t", tag="b_t")
+            nc.vector.scalar_tensor_tensor(
+                out=b_t[i][:], in0=b_sb[i // 4][:, i % 4, :], scalar=0.7, in1=d_t[i][:], op0=ALU.mult, op1=ALU.add
+            )
+
+        def final(i):
+            o_t[i] = work.tile([P, R], F32, name="o_t", tag="o_t", bufs=4)
+            nc.vector.scalar_tensor_tensor(
+                out=o_t[i][:], in0=a_t[i][:], scalar=0.7, in1=b_t[i][:], op0=ALU.mult, op1=ALU.mult
+            )
+            nc.sync.dma_start(out=out_0[P * i : P * (i + 1), :], in_=o_t[i][:])
+
+        def turn(i):
+            bank = ptr.tile([P, 4, P], F32, name="tr2", tag="tr")
+            for t in range(4):
+                nc.tensor.transpose(bank[:, t, :], o_t[i][:, t : R : 4], ident[:])
+            if i % 2 == 0:
+                oi[i // 2] = work.tile([P, 2 * P, 4], BF16, name="oi", tag="oi", bufs=2, align_bytes=64)
+            nc.scalar.copy(
+                out=oi[i // 2][:, P * (i % 2) : P * (i % 2 + 1), :], in_=bank[:].rearrange("p t d -> p d t")
+            )
+
+        def quant_o(i0, n):
+            cols = slice(P * i0, P * (i0 + n))
+            first = i0 % 2
+            nc.vector.quantize_mx(
+                out=o_codes[:, cols].bitcast(E4M3),
+                scales=o_scales[:, cols],
+                in_=oi[i0 // 2][:, P * first : P * (first + n), :].rearrange("p d t -> p (d t)"),
+            )
+            nc.sync.dma_start(
+                out=out_1[0].rearrange("p m t -> p (m t)").bitcast(I32)[:, cols], in_=o_codes[:, cols].bitcast(I32)
+            )
+
+        pieces = [(c, 512) for c in range(NC)] + [(c, 768) for c in range(NC)]
+        per_slot = {-1: 2, 0: 1, 1: 2, 2: 1, 3: 2}
+        made = []
+        stage2(0)
+        for k in range(-1, NB + 1):
+            if k + 1 < NB:
+                prod(k + 1)
+                abs_s(k + 1)
+            if 0 <= k < NB:
+                diff(k)
+                abs_d(k)
+            for c, col in made:
+                quant_x(c, col, 256)
+            made = []
+            if k + 2 < NB:
+                stage2(k + 2)
+            for j in range(per_slot.get(k, 0)):
+                c, col = pieces[0]
+                pieces = pieces[1:]
+                inter_x(c, col, 256)
+                made.append((c, col))
+            if k >= 1:
+                final(k - 1)
+                turn(k - 1)
+            if 0 <= k < NB:
+                i_new(k)
+            if k >= 3 and k % 2 == 1 and k < NB:
+                quant_o(k - 3, 2)
+            if 0 <= k < NB:
+                u_new(k)
+        quant_o(6, 1)
+        quant_o(7, 1)
+        for q in range(4):
+            nc.scalar.dma_start(
+                out=out_2[0, 4 * q : 4 * q + 4, :].bitcast(I32), in_=o_scales[32 * q : 32 * q + 4, :].bitcast(I32)
+            )

@@ -4,8 +4,8 @@ import math
 import concourse.mybir as mybir
 from concourse.masks import make_identity
 
-T, D, F, R = 2048, 1024, 1024, 512
-FLOPS = 2 * T * F * R + 2 * T * D * R
+T_TOTAL, D, F, R = 2048, 1024, 1024, 512
+FLOPS = 2 * T_TOTAL * F * R + 2 * T_TOTAL * D * R
 
 F32 = mybir.dt.float32
 BF16 = mybir.dt.bfloat16
@@ -18,7 +18,7 @@ ALU = mybir.AluOpType
 ACT = mybir.ActivationFunctionType
 
 P = 128
-NC = T // 512
+NC = T_TOTAL // 512
 NB = D // P
 
 
@@ -76,12 +76,13 @@ def tile_adalorasensitivityscore_x2_kernel(
                 out=dst[h][:], in_=src[512 * h : 512 * (h + 1), :].rearrange("(i p) r -> p i r", p=P)
             )
 
+        nc.scalar.activation(out=warm[:], in_=warm[:], func=ACT.Abs)
+        nc.scalar.dma_start(out=lam_sb[:], in_=lam.rearrange("(p m) -> p m", m=4))
         for t in range(4):
             load_g(0, t, t + 1)
         nc.sync.dma_start(
             out=w_words[:].bitcast(I32), in_=q_words.rearrange("g p n -> p g n").bitcast(I32)
         )
-        nc.scalar.dma_start(out=lam_sb[:], in_=lam.rearrange("(p m) -> p m", m=4))
         for q in range(4):
             nc.scalar.dma_start(
                 out=w_scales[32 * q : 32 * q + 4, :, :].bitcast(I32),
@@ -90,201 +91,209 @@ def tile_adalorasensitivityscore_x2_kernel(
         load_g(1, 0, 2)
         load_g(1, 2, 4)
         load_x(0, 0)
-        load_g(2, 0, 4)
+        load_g(2, 0, 2)
+        load_g(2, 2, 4)
         load_x(1, 0)
-        load_g(3, 0, 4)
+        load_g(3, 0, 2)
+        load_g(3, 2, 4)
         load_x(2, 0)
         load_x(3, 0)
+        for c in range(3):
+            load_x(c, 1)
         load_e(p_sb, p, 0)
         load_e(a_sb, avg_i, 0)
         load_e(b_sb, avg_u, 0)
-        for c in range(NC):
-            load_x(c, 1)
+        load_x(3, 1)
         load_e(p_sb, p, 1)
         load_e(a_sb, avg_i, 1)
         load_e(b_sb, avg_u, 1)
 
-        nc.scalar.activation(out=warm[:], in_=warm[:], func=ACT.Abs)
+        gi, acc, ui, xi, tr = {}, {}, {}, {}, {}
+        gacc, s_t, d_t, a_t, b_t, o_t, oi = {}, {}, {}, {}, {}, {}, {}
+        na_t, bt_t, dbank, bbank = {}, {}, {}, {}
 
-        gi = {}
+        def T(c, t):
+            bank = ptr.tile([P, 2, 2, P], F32, name="tr", tag="tr")
+            words = g_sb[c][:, t, :].bitcast(F32)
+            for k in range(2):
+                for u in range(2):
+                    nc.tensor.transpose(bank[:, k, u, :], words[:, 256 * k + u : 256 * (k + 1) : 2], ident[:])
+            tr[c, t] = bank
 
-        def transposes(c):
+        def GC(c, t):
+            bank = tr[c, t]
+            if (c, t // 2) not in gi:
+                gi[c, t // 2] = work.tile([P, 2048], BF16, name="gi", tag="gi", bufs=5, align_bytes=64)
+            dst = gi[c, t // 2][:].bitcast(F32)[:, 512 * (t % 2) : 512 * (t % 2 + 1)]
+            nc.scalar.copy(
+                out=dst.rearrange("p (k r u) -> p k r u", k=2, u=2), in_=bank[:].rearrange("p k u r -> p k r u")
+            )
+
+        def LAM():
+            lbank = pacc.tile([P, 4, P], BF16, name="lbank", tag="acc")
+            for m in range(4):
+                nc.tensor.transpose(lbank[:, m, :], lam_sb[:, m : m + 1].to_broadcast([P, P]), ident16[:])
+            tr[0] = lbank
+
+        def LC():
+            lbank = tr[0]
+            nc.scalar.copy(
+                out=lam_bc[:].rearrange("p (n m) -> p n m", m=4), in_=lbank[:].rearrange("p m n -> p n m")
+            )
+
+        def QG(c, h):
+            nc.vector.quantize_mx(
+                out=g_codes[c][:, 512 * h : 512 * (h + 1)].bitcast(E4M3),
+                scales=g_scales[c][:, 512 * h : 512 * (h + 1)],
+                in_=gi[c, h][:],
+            )
+
+        def M(c, rb):
+            bank = pacc.tile([P, 512], F32, name="acc", tag="acc")
+            acc[c, rb] = bank
             for t in range(4):
-                if t % 2 == 0:
-                    gi[c, t // 2] = work.tile([P, 2048], BF16, name="gi", tag="gi", align_bytes=64)
-                bank = ptr.tile([P, 2, 2, P], F32, name="tr", tag="tr")
-                words = g_sb[c][:, t, :].bitcast(F32)
                 for k in range(2):
-                    for u in range(2):
-                        nc.tensor.transpose(
-                            bank[:, k, u, :], words[:, 256 * k + u : 256 * (k + 1) : 2], ident[:]
-                        )
-                dst = gi[c, t // 2][:].bitcast(F32)[:, 512 * (t % 2) : 512 * (t % 2 + 1)]
-                nc.scalar.copy(
-                    out=dst.rearrange("p (k r u) -> p k r u", k=2, u=2),
-                    in_=bank[:].rearrange("p k u r -> p k r u"),
-                )
+                    cols = slice((2 * t + k) * P, (2 * t + k + 1) * P)
+                    nc.tensor.matmul_mx(
+                        out=bank[:, P * t : P * (t + 1)],
+                        lhsT=g_codes[c][:, cols].bitcast(E4M3),
+                        lhsT_scale=g_scales[c][:, cols],
+                        rhs=w_words[:, k, 256 * rb : 256 * (rb + 1)].bitcast(E2M1),
+                        rhs_scale=w_scales[:, k, P * rb : P * (rb + 1)],
+                        start=(k == 0),
+                        stop=(k == 1),
+                    )
 
-        def quant_g(c):
-            for h in range(2):
-                nc.vector.quantize_mx(
-                    out=g_codes[c][:, 512 * h : 512 * (h + 1)].bitcast(E4M3),
-                    scales=g_scales[c][:, 512 * h : 512 * (h + 1)],
-                    in_=gi[c, h][:],
-                )
+        def L(c, rb):
+            if c not in ui:
+                ui[c] = work.tile([P, R, 4], BF16, name="ui", tag="gi", bufs=5, align_bytes=64)
+            rs = slice(P * rb, P * (rb + 1))
+            nc.vector.tensor_tensor(
+                out=ui[c][:, rs, :],
+                in0=acc[c, rb][:].rearrange("p (t n) -> p n t", t=4),
+                in1=lam_bc[:, rs].unsqueeze(2).to_broadcast([P, P, 4]),
+                op=ALU.mult,
+            )
 
-        acc = {}
-
-        def stage1(c):
-            for rb in range(4):
-                bank = pacc.tile([P, 512], F32, name="acc", tag="acc")
-                acc[c, rb] = bank
-                for t in range(4):
-                    for k in range(2):
-                        cols = slice((2 * t + k) * P, (2 * t + k + 1) * P)
-                        nc.tensor.matmul_mx(
-                            out=bank[:, P * t : P * (t + 1)],
-                            lhsT=g_codes[c][:, cols].bitcast(E4M3),
-                            lhsT_scale=g_scales[c][:, cols],
-                            rhs=w_words[:, k, 256 * rb : 256 * (rb + 1)].bitcast(E2M1),
-                            rhs_scale=w_scales[:, k, P * rb : P * (rb + 1)],
-                            start=(k == 0),
-                            stop=(k == 1),
-                        )
-
-        ui = {}
-
-        def times_lam(c):
-            ui[c] = work.tile([P, R, 4], BF16, name="ui", tag="ui", bufs=2, align_bytes=64)
-            for rb in range(4):
-                rs = slice(P * rb, P * (rb + 1))
-                nc.vector.tensor_tensor(
-                    out=ui[c][:, rs, :],
-                    in0=acc[c, rb][:].rearrange("p (t n) -> p n t", t=4),
-                    in1=lam_bc[:, rs].unsqueeze(2).to_broadcast([P, P, 4]),
-                    op=ALU.mult,
-                )
-
-        def quant_u(c):
+        def QU(c):
             nc.vector.quantize_mx(
                 out=u_codes[c][:].bitcast(E4M3), scales=u_scales[c][:], in_=ui[c][:].rearrange("p n t -> p (n t)")
             )
 
-        xi = {}
+        def XI(c, q, eng="S"):
+            h, o = q // 2, 256 * (q % 2)
+            t = work.tile([P, 256, 4], BF16, name="xi", tag="xi", bufs=6, align_bytes=64)
+            xi[c, q] = t
+            dst = t[:].rearrange("p (d i) t -> p d t i", i=4)
+            view = x_sb[c][h][:, :, o : o + 256].rearrange("p t (d i) -> p d t i", i=4)
+            if eng == "S":
+                nc.scalar.copy(out=dst, in_=view)
+            elif eng == "V":
+                nc.vector.tensor_copy(out=dst, in_=view)
+            else:
+                nc.gpsimd.tensor_scalar(out=dst, in0=view, scalar1=1.0, scalar2=0.0, op0=ALU.mult, op1=ALU.add)
 
-        def inter_x(c, col, width):
-            h, o = col // 512, col % 512
-            t = work.tile([P, width, 4], BF16, name="xi%d" % width, tag="xi%d" % width, align_bytes=64)
-            xi[c, col] = t
-            for s in range(0, width, 256):
-                nc.scalar.copy(
-                    out=t[:, s : s + 256, :],
-                    in_=x_sb[c][h][:, :, o + s : o + s + 256].rearrange("p t d -> p d t"),
-                )
-
-        def quant_x(c, col, width):
+        def QX(c, q):
             nc.vector.quantize_mx(
-                out=x_codes[c][:, col : col + width].bitcast(E4M3),
-                scales=x_scales[c][:, col : col + width],
-                in_=xi[c, col][:].rearrange("p d t -> p (d t)"),
+                out=x_codes[c][:, 256 * q : 256 * (q + 1)].bitcast(E4M3),
+                scales=x_scales[c][:, 256 * q : 256 * (q + 1)],
+                in_=xi[c, q][:].rearrange("p d t -> p (d t)"),
             )
 
-        transposes(0)
-        lbank = pacc.tile([P, 4, P], BF16, name="lbank", tag="acc")
-        for m in range(4):
-            nc.tensor.transpose(lbank[:, m, :], lam_sb[:, m : m + 1].to_broadcast([P, P]), ident16[:])
-        nc.scalar.copy(
-            out=lam_bc[:].rearrange("p (n m) -> p n m", m=4), in_=lbank[:].rearrange("p m n -> p n m")
-        )
-        quant_g(0)
-        transposes(1)
-        quant_g(1)
-        stage1(0)
-        inter_x(0, 0, 512)
-        times_lam(0)
-        transposes(2)
-        quant_x(0, 0, 512)
-        quant_u(0)
-        quant_g(2)
-        stage1(1)
-        inter_x(1, 0, 512)
-        times_lam(1)
-        transposes(3)
-        quant_x(1, 0, 512)
-        quant_u(1)
-        quant_g(3)
-        stage1(2)
-        inter_x(2, 0, 512)
-        times_lam(2)
-        stage1(3)
-        inter_x(3, 0, 512)
-        quant_x(2, 0, 512)
-        quant_u(2)
-        times_lam(3)
-        quant_x(3, 0, 512)
-        quant_u(3)
-
-        gacc, s_t, d_t, a_t, b_t, o_t, oi = {}, {}, {}, {}, {}, {}, {}
-
-        def stage2(i):
-            bank = pacc.tile([P, 512], F32, name="acc2", tag="acc")
-            gacc[i] = bank
+        def N(i, c):
+            if c == 0:
+                gacc[i] = pacc.tile([P, 512], F32, name="acc2", tag="acc")
             cols = slice(P * i, P * (i + 1))
-            for c in range(NC):
-                nc.tensor.matmul_mx(
-                    out=bank[:],
-                    lhsT=x_codes[c][:, cols].bitcast(E4M3),
-                    lhsT_scale=x_scales[c][:, cols],
-                    rhs=u_codes[c][:].bitcast(E4M3),
-                    rhs_scale=u_scales[c][:],
-                    start=(c == 0),
-                    stop=(c == NC - 1),
-                )
+            nc.tensor.matmul_mx(
+                out=gacc[i][:],
+                lhsT=x_codes[c][:, cols].bitcast(E4M3),
+                lhsT_scale=x_scales[c][:, cols],
+                rhs=u_codes[c][:].bitcast(E4M3),
+                rhs_scale=u_scales[c][:],
+                start=(c == 0),
+                stop=(c == NC - 1),
+            )
 
-        def prod(i):
-            s_t[i] = work.tile([P, R], F32, name="s_t", tag="s_t")
+        def PR(i):
+            s_t[i] = work.tile([P, R], F32, name="s_t", tag="s_t", bufs=6)
             nc.vector.tensor_tensor(out=s_t[i][:], in0=gacc[i][:], in1=p_sb[i // 4][:, i % 4, :], op=ALU.mult)
 
-        def abs_s(i):
-            nc.scalar.activation(out=s_t[i][:], in_=s_t[i][:], func=ACT.Abs, scale=1.0 / math.sqrt(T))
+        def S1(i):
+            nc.scalar.activation(out=s_t[i][:], in_=s_t[i][:], func=ACT.Abs, scale=1.0 / math.sqrt(T_TOTAL))
 
-        def diff(i):
-            d_t[i] = work.tile([P, R], F32, name="d_t", tag="d_t")
+        def DF(i):
+            d_t[i] = work.tile([P, R], F32, name="d_t", tag="d_t", bufs=4)
             nc.vector.tensor_tensor(out=d_t[i][:], in0=s_t[i][:], in1=a_sb[i // 4][:, i % 4, :], op=ALU.subtract)
 
-        def abs_d(i):
-            nc.scalar.activation(out=d_t[i][:], in_=d_t[i][:], func=ACT.Abs, scale=0.21)
+        def S2(i):
+            nc.scalar.activation(out=d_t[i][:], in_=d_t[i][:], func=ACT.Abs, scale=0.3)
 
-        def i_new(i):
-            a_t[i] = work.tile([P, R], F32, name="a_t", tag="a_t")
+        def A(i):
+            a_t[i] = work.tile([P, R], F32, name="a_t", tag="a_t", bufs=4)
             nc.vector.scalar_tensor_tensor(
                 out=a_t[i][:], in0=s_t[i][:], scalar=0.3 / 0.7, in1=a_sb[i // 4][:, i % 4, :], op0=ALU.mult, op1=ALU.add
             )
 
-        def u_new(i):
-            b_t[i] = work.tile([P, R], F32, name="b_t", tag="b_t")
-            nc.vector.scalar_tensor_tensor(
-                out=b_t[i][:], in0=b_sb[i // 4][:, i % 4, :], scalar=0.7, in1=d_t[i][:], op0=ALU.mult, op1=ALU.add
-            )
+        def B(i):
+            b_t[i] = work.tile([P, R], F32, name="b_t", tag="b_t", bufs=4)
+            nc.vector.tensor_tensor(out=b_t[i][:], in0=d_t[i][:], in1=b_sb[i // 4][:, i % 4, :], op=ALU.add)
 
-        def final(i):
+        def O(i):
             o_t[i] = work.tile([P, R], F32, name="o_t", tag="o_t", bufs=4)
+            second = b_t[i] if i in b_t else bbank[i]
             nc.vector.scalar_tensor_tensor(
-                out=o_t[i][:], in0=a_t[i][:], scalar=0.7, in1=b_t[i][:], op0=ALU.mult, op1=ALU.mult
+                out=o_t[i][:], in0=a_t[i][:], scalar=0.49, in1=second[:], op0=ALU.mult, op1=ALU.mult
             )
             nc.sync.dma_start(out=out_0[P * i : P * (i + 1), :], in_=o_t[i][:])
 
-        def turn(i):
+        def NEG(i):
+            na_t[i] = work.tile([P, R], F32, name="na_t", tag="na_t", bufs=2)
+            nc.gpsimd.tensor_scalar(out=na_t[i][:], in0=a_sb[i // 4][:, i % 4, :], scalar1=-1.0, scalar2=0.0, op0=ALU.mult, op1=ALU.add)
+
+        def BT(i):
+            bank = ptr.tile([P, 4, P], BF16, name="tr3", tag="tr")
+            for q in range(4):
+                nc.tensor.transpose(bank[:, q, :], b_sb[i // 4][:, i % 4, P * q : P * (q + 1)], ident16[:])
+            tr["b", i] = bank
+
+        def BC(i):
+            bt_t[i] = work.tile([P, 4, P], F32, name="bt_t", tag="bt_t", bufs=2)
+            nc.scalar.copy(out=bt_t[i][:], in_=tr["b", i][:])
+
+        def DT(i):
+            bank = ptr.tile([P, 4, P], F32, name="tr4", tag="tr")
+            for q in range(4):
+                cols = slice(P * q, P * (q + 1))
+                nc.tensor.matmul(bank[:, q, :], s_t[i][:, cols], ident[:], start=True, stop=False, is_transpose=True)
+                nc.tensor.matmul(bank[:, q, :], na_t[i][:, cols], ident[:], start=False, stop=True, is_transpose=True)
+            dbank[i] = bank
+
+        def E2(i):
+            d_t[i] = work.tile([P, 4, P], F32, name="e_t", tag="d_t", bufs=4)
+            nc.scalar.activation(out=d_t[i][:], in_=dbank[i][:], func=ACT.Abs, scale=0.3)
+
+        def BP(i):
+            bank = ptr.tile([P, 4, P], F32, name="tr5", tag="tr")
+            for q in range(4):
+                nc.tensor.matmul(bank[:, q, :], d_t[i][:, q, :], ident[:], start=True, stop=False, is_transpose=True)
+                nc.tensor.matmul(bank[:, q, :], bt_t[i][:, q, :], ident[:], start=False, stop=True, is_transpose=True)
+            bbank[i] = bank[:].rearrange("p q r -> p (q r)")
+
+        def OT(i):
             bank = ptr.tile([P, 4, P], F32, name="tr2", tag="tr")
             for t in range(4):
                 nc.tensor.transpose(bank[:, t, :], o_t[i][:, t : R : 4], ident[:])
-            if i % 2 == 0:
-                oi[i // 2] = work.tile([P, 2 * P, 4], BF16, name="oi", tag="oi", bufs=2, align_bytes=64)
+            tr["o", i] = bank
+
+        def OC(i):
+            bank = tr["o", i]
+            if i // 2 not in oi:
+                oi[i // 2] = work.tile([P, 2 * P, 4], BF16, name="oi", tag="gi", bufs=5, align_bytes=64)
             nc.scalar.copy(
                 out=oi[i // 2][:, P * (i % 2) : P * (i % 2 + 1), :], in_=bank[:].rearrange("p t d -> p d t")
             )
 
-        def quant_o(i0, n):
+        def QO(i0, n):
             cols = slice(P * i0, P * (i0 + n))
             first = i0 % 2
             nc.vector.quantize_mx(
@@ -296,39 +305,236 @@ def tile_adalorasensitivityscore_x2_kernel(
                 out=out_1[0].rearrange("p m t -> p (m t)").bitcast(I32)[:, cols], in_=o_codes[:, cols].bitcast(I32)
             )
 
-        pieces = [(c, 512) for c in range(NC)] + [(c, 768) for c in range(NC)]
-        per_slot = {-1: 2, 0: 1, 1: 2, 2: 1, 3: 2}
-        made = []
-        stage2(0)
-        for k in range(-1, NB + 1):
-            if k + 1 < NB:
-                prod(k + 1)
-                abs_s(k + 1)
-            if 0 <= k < NB:
-                diff(k)
-                abs_d(k)
-            for c, col in made:
-                quant_x(c, col, 256)
-            made = []
-            if k + 2 < NB:
-                stage2(k + 2)
-            for j in range(per_slot.get(k, 0)):
-                c, col = pieces[0]
-                pieces = pieces[1:]
-                inter_x(c, col, 256)
-                made.append((c, col))
-            if k >= 1:
-                final(k - 1)
-                turn(k - 1)
-            if 0 <= k < NB:
-                i_new(k)
-            if k >= 3 and k % 2 == 1 and k < NB:
-                quant_o(k - 3, 2)
-            if 0 <= k < NB:
-                u_new(k)
-        quant_o(6, 1)
-        quant_o(7, 1)
-        for q in range(4):
-            nc.scalar.dma_start(
-                out=out_2[0, 4 * q : 4 * q + 4, :].bitcast(I32), in_=o_scales[32 * q : 32 * q + 4, :].bitcast(I32)
-            )
+        def SC(lo, hi):
+            for q in range(4):
+                nc.scalar.dma_start(
+                    out=out_2[0, 4 * q : 4 * q + 4, lo:hi].bitcast(I32),
+                    in_=o_scales[32 * q : 32 * q + 4, lo:hi].bitcast(I32),
+                )
+
+        LAM()
+        T(0, 0)
+        T(0, 2)
+        GC(0, 0)
+        GC(0, 2)
+        T(0, 1)
+        T(0, 3)
+        GC(0, 1)
+        QG(0, 0)
+        GC(0, 3)
+        T(1, 0)
+        T(1, 1)
+        QG(0, 1)
+        T(1, 2)
+        LC()
+        M(0, 0)
+        M(0, 3)
+        M(0, 2)
+        M(0, 1)
+        GC(1, 0)
+        T(1, 3)
+        T(2, 0)
+        L(0, 0)
+        GC(1, 1)
+        QG(1, 0)
+        GC(1, 2)
+        T(2, 2)
+        XI(0, 1, "S")
+        L(0, 2)
+        XI(0, 0, "S")
+        GC(1, 3)
+        L(0, 1)
+        GC(2, 0)
+        T(2, 1)
+        L(0, 3)
+        GC(2, 2)
+        QG(1, 1)
+        GC(2, 1)
+        XI(1, 1, "S")
+        QU(0)
+        T(2, 3)
+        M(1, 0)
+        M(1, 3)
+        M(1, 2)
+        GC(2, 3)
+        QX(0, 0)
+        QG(2, 0)
+        M(1, 1)
+        L(1, 0)
+        XI(2, 0, "S")
+        L(1, 3)
+        QG(2, 1)
+        T(3, 1)
+        T(3, 0)
+        XI(1, 0, "S")
+        L(1, 1)
+        T(3, 2)
+        L(1, 2)
+        T(3, 3)
+        M(2, 0)
+        QX(2, 0)
+        M(2, 2)
+        GC(3, 2)
+        QX(0, 1)
+        GC(3, 0)
+        QX(1, 1)
+        QX(1, 0)
+        QU(1)
+        L(2, 0)
+        GC(3, 3)
+        QG(3, 1)
+        M(2, 3)
+        GC(3, 1)
+        M(2, 1)
+        XI(3, 1, "S")
+        QG(3, 0)
+        NEG(1)
+        NEG(4)
+        M(3, 0)
+        L(2, 3)
+        L(2, 2)
+        L(3, 0)
+        L(2, 1)
+        M(3, 1)
+        L(3, 1)
+        M(3, 3)
+        M(3, 2)
+        L(3, 3)
+        QX(3, 1)
+        L(3, 2)
+        XI(3, 0, "S")
+        N(0, 0)
+        XI(2, 1, "S")
+        QU(2)
+        QX(2, 1)
+        N(2, 0)
+        BT(1)
+        QU(3)
+        XI(0, 3, "S")
+        N(0, 1)
+        QX(0, 3)
+        N(3, 0)
+        N(1, 0)
+        XI(1, 2, "S")
+        N(2, 1)
+        N(2, 2)
+        N(3, 1)
+        XI(2, 3, "S")
+        N(3, 2)
+        N(3, 3)
+        QX(3, 0)
+        XI(0, 2, "S")
+        N(0, 2)
+        QX(1, 2)
+        N(2, 3)
+        PR(3)
+        N(1, 1)
+        PR(2)
+        N(0, 3)
+        PR(0)
+        N(1, 2)
+        BT(4)
+        S1(3)
+        QX(2, 3)
+        QX(0, 2)
+        S1(2)
+        N(1, 3)
+        PR(1)
+        XI(2, 2, "S")
+        S1(0)
+        DF(3)
+        DF(2)
+        S2(2)
+        N(7, 0)
+        S2(3)
+        S1(1)
+        A(3)
+        XI(1, 3, "S")
+        A(2)
+        N(6, 0)
+        QX(2, 2)
+        B(2)
+        DF(0)
+        XI(3, 2, "S")
+        N(5, 0)
+        N(5, 1)
+        B(3)
+        N(5, 2)
+        O(2)
+        O(3)
+        N(4, 0)
+        N(4, 1)
+        DT(1)
+        S2(0)
+        XI(3, 3, "S")
+        QX(1, 3)
+        OT(2)
+        A(1)
+        N(7, 1)
+        N(7, 2)
+        A(0)
+        BC(1)
+        B(0)
+        N(4, 2)
+        E2(1)
+        N(6, 1)
+        QX(3, 2)
+        N(6, 2)
+        N(5, 3)
+        O(0)
+        N(4, 3)
+        QX(3, 3)
+        N(7, 3)
+        N(6, 3)
+        BP(1)
+        PR(5)
+        PR(4)
+        BC(4)
+        PR(7)
+        PR(6)
+        S1(5)
+        O(1)
+        S1(4)
+        DT(4)
+        S1(7)
+        OC(2)
+        E2(4)
+        DF(5)
+        DF(7)
+        OT(3)
+        A(4)
+        OT(1)
+        S1(6)
+        S2(7)
+        A(7)
+        A(5)
+        OC(3)
+        S2(5)
+        DF(6)
+        S2(6)
+        B(5)
+        BP(4)
+        OT(0)
+        O(4)
+        OC(0)
+        B(7)
+        A(6)
+        OC(1)
+        O(5)
+        OT(4)
+        OT(5)
+        OC(4)
+        O(7)
+        OT(7)
+        B(6)
+        O(6)
+        OC(7)
+        QO(7, 1)
+        OC(5)
+        QO(2, 2)
+        OT(6)
+        QO(0, 2)
+        OC(6)
+        QO(4, 2)
+        QO(6, 1)
+        SC(0, D)

from contextlib import ExitStack
import math

import concourse.mybir as mybir
from concourse.masks import make_identity

T_TOTAL, D, F, R = 2048, 1024, 1024, 512
FLOPS = 2 * T_TOTAL * F * R + 2 * T_TOTAL * D * R

F32 = mybir.dt.float32
BF16 = mybir.dt.bfloat16
I32 = mybir.dt.int32
U32 = mybir.dt.uint32
U8 = mybir.dt.uint8
E4M3 = mybir.dt.float8_e4m3fn_x4
E2M1 = mybir.dt.float4_e2m1fn_x4
ALU = mybir.AluOpType
ACT = mybir.ActivationFunctionType

P = 128
NC = T_TOTAL // 512
NB = D // P


def tile_adalorasensitivityscore_x2_kernel(
    tc, x, g, p, lam, q_words, q_scales, avg_i, avg_u, out_0, out_1, out_2
):
    nc = tc.nc
    with ExitStack() as ctx:
        keep = ctx.enter_context(tc.tile_pool(name="keep", bufs=1))
        work = ctx.enter_context(tc.tile_pool(name="work", bufs=3))
        ptr = ctx.enter_context(tc.psum_pool(name="ptr", bufs=4))
        pacc = ctx.enter_context(tc.psum_pool(name="pacc", bufs=4))
        ctx.enter_context(tc.manual_schedule())

        g_sb = [keep.tile([P, 4, F], BF16, name="g%d" % c) for c in range(NC)]
        x_sb = [[keep.tile([P, 4, 512], BF16, name="x%d_%d" % (c, h)) for h in range(2)] for c in range(NC)]
        w_words = keep.tile([P, 2, 2 * R], U8, name="w_words", align_bytes=64)
        w_scales = keep.tile([P, 2, R], U8, name="w_scales", align_bytes=64)
        g_codes = [keep.tile([P, 1024], U32, name="gc%d" % c, align_bytes=64) for c in range(NC)]
        g_scales = [keep.tile([P, 1024], U8, name="gs%d" % c, align_bytes=64) for c in range(NC)]
        u_codes = [keep.tile([P, R], U32, name="uc%d" % c, align_bytes=64) for c in range(NC)]
        u_scales = [keep.tile([P, R], U8, name="us%d" % c, align_bytes=64) for c in range(NC)]
        x_codes = [keep.tile([P, D], U32, name="xc%d" % c, align_bytes=64) for c in range(NC)]
        x_scales = [keep.tile([P, D], U8, name="xs%d" % c, align_bytes=64) for c in range(NC)]
        o_codes = keep.tile([P, D], U32, name="o_codes", align_bytes=64)
        o_scales = keep.tile([P, D], U8, name="o_scales", align_bytes=64)
        p_sb = [keep.tile([P, 4, R], BF16, name="p%d" % h) for h in range(2)]
        a_sb = [keep.tile([P, 4, R], BF16, name="a%d" % h) for h in range(2)]
        b_sb = [keep.tile([P, 4, R], BF16, name="b%d" % h) for h in range(2)]
        ident = keep.tile([P, P], F32, name="ident")
        ident16 = keep.tile([P, P], BF16, name="ident16")
        lam_sb = keep.tile([P, 4], BF16, name="lam_sb")
        lam_bc = keep.tile([P, R], BF16, name="lam_bc")
        warm = keep.tile([P, 1], F32, name="warm")

        nc.vector.memset(w_scales[:].bitcast(I32), 0)
        nc.vector.memset(warm[:], 1.0)
        make_identity(nc, ident[:])
        make_identity(nc, ident16[:])

        def load_g(c, t0, t1):
            nc.sync.dma_start(
                out=g_sb[c][:, t0:t1, :],
                in_=g[512 * c : 512 * (c + 1), :].rearrange("(p t) f -> p t f", t=4)[:, t0:t1, :],
            )

        def load_x(c, h):
            nc.sync.dma_start(
                out=x_sb[c][h][:],
                in_=x[512 * c : 512 * (c + 1), 512 * h : 512 * (h + 1)].rearrange("(p t) f -> p t f", t=4),
            )

        def load_e(dst, src, h):
            nc.sync.dma_start(
                out=dst[h][:], in_=src[512 * h : 512 * (h + 1), :].rearrange("(i p) r -> p i r", p=P)
            )

        nc.scalar.activation(out=warm[:], in_=warm[:], func=ACT.Abs)
        nc.scalar.dma_start(out=lam_sb[:], in_=lam.rearrange("(p m) -> p m", m=4))
        for t in range(4):
            load_g(0, t, t + 1)
        nc.sync.dma_start(
            out=w_words[:].bitcast(I32), in_=q_words.rearrange("g p n -> p g n").bitcast(I32)
        )
        for q in range(4):
            nc.scalar.dma_start(
                out=w_scales[32 * q : 32 * q + 4, :, :].bitcast(I32),
                in_=q_scales[:, 4 * q : 4 * q + 4, :].rearrange("g q n -> q g n").bitcast(I32),
            )
        load_g(1, 0, 2)
        load_g(1, 2, 4)
        load_x(0, 0)
        load_g(2, 0, 2)
        load_g(2, 2, 4)
        load_x(1, 0)
        load_g(3, 0, 2)
        load_g(3, 2, 4)
        load_x(2, 0)
        load_x(3, 0)
        for c in range(3):
            load_x(c, 1)
        load_e(p_sb, p, 0)
        load_e(a_sb, avg_i, 0)
        load_e(b_sb, avg_u, 0)
        load_x(3, 1)
        load_e(p_sb, p, 1)
        load_e(a_sb, avg_i, 1)
        load_e(b_sb, avg_u, 1)

        gi, acc, ui, xi, tr = {}, {}, {}, {}, {}
        gacc, s_t, d_t, a_t, b_t, o_t, oi = {}, {}, {}, {}, {}, {}, {}
        na_t, bt_t, dbank, bbank = {}, {}, {}, {}

        def T(c, t):
            bank = ptr.tile([P, 2, 2, P], F32, name="tr", tag="tr")
            words = g_sb[c][:, t, :].bitcast(F32)
            for k in range(2):
                for u in range(2):
                    nc.tensor.transpose(bank[:, k, u, :], words[:, 256 * k + u : 256 * (k + 1) : 2], ident[:])
            tr[c, t] = bank

        def GC(c, t):
            bank = tr[c, t]
            if (c, t // 2) not in gi:
                gi[c, t // 2] = work.tile([P, 2048], BF16, name="gi", tag="gi", bufs=5, align_bytes=64)
            dst = gi[c, t // 2][:].bitcast(F32)[:, 512 * (t % 2) : 512 * (t % 2 + 1)]
            nc.scalar.copy(
                out=dst.rearrange("p (k r u) -> p k r u", k=2, u=2), in_=bank[:].rearrange("p k u r -> p k r u")
            )

        def LAM():
            lbank = pacc.tile([P, 4, P], BF16, name="lbank", tag="acc")
            for m in range(4):
                nc.tensor.transpose(lbank[:, m, :], lam_sb[:, m : m + 1].to_broadcast([P, P]), ident16[:])
            tr[0] = lbank

        def LC():
            lbank = tr[0]
            nc.scalar.copy(
                out=lam_bc[:].rearrange("p (n m) -> p n m", m=4), in_=lbank[:].rearrange("p m n -> p n m")
            )

        def QG(c, h):
            nc.vector.quantize_mx(
                out=g_codes[c][:, 512 * h : 512 * (h + 1)].bitcast(E4M3),
                scales=g_scales[c][:, 512 * h : 512 * (h + 1)],
                in_=gi[c, h][:],
            )

        def M(c, rb):
            bank = pacc.tile([P, 512], F32, name="acc", tag="acc")
            acc[c, rb] = bank
            for t in range(4):
                for k in range(2):
                    cols = slice((2 * t + k) * P, (2 * t + k + 1) * P)
                    nc.tensor.matmul_mx(
                        out=bank[:, P * t : P * (t + 1)],
                        lhsT=g_codes[c][:, cols].bitcast(E4M3),
                        lhsT_scale=g_scales[c][:, cols],
                        rhs=w_words[:, k, 256 * rb : 256 * (rb + 1)].bitcast(E2M1),
                        rhs_scale=w_scales[:, k, P * rb : P * (rb + 1)],
                        start=(k == 0),
                        stop=(k == 1),
                    )

        def L(c, rb):
            if c not in ui:
                ui[c] = work.tile([P, R, 4], BF16, name="ui", tag="gi", bufs=5, align_bytes=64)
            rs = slice(P * rb, P * (rb + 1))
            nc.vector.tensor_tensor(
                out=ui[c][:, rs, :],
                in0=acc[c, rb][:].rearrange("p (t n) -> p n t", t=4),
                in1=lam_bc[:, rs].unsqueeze(2).to_broadcast([P, P, 4]),
                op=ALU.mult,
            )

        def QU(c):
            nc.vector.quantize_mx(
                out=u_codes[c][:].bitcast(E4M3), scales=u_scales[c][:], in_=ui[c][:].rearrange("p n t -> p (n t)")
            )

        def XI(c, q, eng="S"):
            h, o = q // 2, 256 * (q % 2)
            t = work.tile([P, 256, 4], BF16, name="xi", tag="xi", bufs=6, align_bytes=64)
            xi[c, q] = t
            dst = t[:].rearrange("p (d i) t -> p d t i", i=4)
            view = x_sb[c][h][:, :, o : o + 256].rearrange("p t (d i) -> p d t i", i=4)
            if eng == "S":
                nc.scalar.copy(out=dst, in_=view)
            elif eng == "V":
                nc.vector.tensor_copy(out=dst, in_=view)
            else:
                nc.gpsimd.tensor_scalar(out=dst, in0=view, scalar1=1.0, scalar2=0.0, op0=ALU.mult, op1=ALU.add)

        def QX(c, q):
            nc.vector.quantize_mx(
                out=x_codes[c][:, 256 * q : 256 * (q + 1)].bitcast(E4M3),
                scales=x_scales[c][:, 256 * q : 256 * (q + 1)],
                in_=xi[c, q][:].rearrange("p d t -> p (d t)"),
            )

        def N(i, c):
            if c == 0:
                gacc[i] = pacc.tile([P, 512], F32, name="acc2", tag="acc")
            cols = slice(P * i, P * (i + 1))
            nc.tensor.matmul_mx(
                out=gacc[i][:],
                lhsT=x_codes[c][:, cols].bitcast(E4M3),
                lhsT_scale=x_scales[c][:, cols],
                rhs=u_codes[c][:].bitcast(E4M3),
                rhs_scale=u_scales[c][:],
                start=(c == 0),
                stop=(c == NC - 1),
            )

        def PR(i):
            s_t[i] = work.tile([P, R], F32, name="s_t", tag="s_t", bufs=6)
            nc.vector.tensor_tensor(out=s_t[i][:], in0=gacc[i][:], in1=p_sb[i // 4][:, i % 4, :], op=ALU.mult)

        def S1(i):
            nc.scalar.activation(out=s_t[i][:], in_=s_t[i][:], func=ACT.Abs, scale=1.0 / math.sqrt(T_TOTAL))

        def DF(i):
            d_t[i] = work.tile([P, R], F32, name="d_t", tag="d_t", bufs=4)
            nc.vector.tensor_tensor(out=d_t[i][:], in0=s_t[i][:], in1=a_sb[i // 4][:, i % 4, :], op=ALU.subtract)

        def S2(i):
            nc.scalar.activation(out=d_t[i][:], in_=d_t[i][:], func=ACT.Abs, scale=0.3)

        def A(i):
            a_t[i] = work.tile([P, R], F32, name="a_t", tag="a_t", bufs=4)
            nc.vector.scalar_tensor_tensor(
                out=a_t[i][:], in0=s_t[i][:], scalar=0.3 / 0.7, in1=a_sb[i // 4][:, i % 4, :], op0=ALU.mult, op1=ALU.add
            )

        def B(i):
            b_t[i] = work.tile([P, R], F32, name="b_t", tag="b_t", bufs=4)
            nc.vector.tensor_tensor(out=b_t[i][:], in0=d_t[i][:], in1=b_sb[i // 4][:, i % 4, :], op=ALU.add)

        def O(i):
            o_t[i] = work.tile([P, R], F32, name="o_t", tag="o_t", bufs=4)
            second = b_t[i] if i in b_t else bbank[i]
            nc.vector.scalar_tensor_tensor(
                out=o_t[i][:], in0=a_t[i][:], scalar=0.49, in1=second[:], op0=ALU.mult, op1=ALU.mult
            )
            nc.sync.dma_start(out=out_0[P * i : P * (i + 1), :], in_=o_t[i][:])

        def NEG(i):
            na_t[i] = work.tile([P, R], F32, name="na_t", tag="na_t", bufs=2)
            nc.gpsimd.tensor_scalar(out=na_t[i][:], in0=a_sb[i // 4][:, i % 4, :], scalar1=-1.0, scalar2=0.0, op0=ALU.mult, op1=ALU.add)

        def BT(i):
            bank = ptr.tile([P, 4, P], BF16, name="tr3", tag="tr")
            for q in range(4):
                nc.tensor.transpose(bank[:, q, :], b_sb[i // 4][:, i % 4, P * q : P * (q + 1)], ident16[:])
            tr["b", i] = bank

        def BC(i):
            bt_t[i] = work.tile([P, 4, P], F32, name="bt_t", tag="bt_t", bufs=2)
            nc.scalar.copy(out=bt_t[i][:], in_=tr["b", i][:])

        def DT(i):
            bank = ptr.tile([P, 4, P], F32, name="tr4", tag="tr")
            for q in range(4):
                cols = slice(P * q, P * (q + 1))
                nc.tensor.matmul(bank[:, q, :], s_t[i][:, cols], ident[:], start=True, stop=False, is_transpose=True)
                nc.tensor.matmul(bank[:, q, :], na_t[i][:, cols], ident[:], start=False, stop=True, is_transpose=True)
            dbank[i] = bank

        def E2(i):
            d_t[i] = work.tile([P, 4, P], F32, name="e_t", tag="d_t", bufs=4)
            nc.scalar.activation(out=d_t[i][:], in_=dbank[i][:], func=ACT.Abs, scale=0.3)

        def BP(i):
            bank = ptr.tile([P, 4, P], F32, name="tr5", tag="tr")
            for q in range(4):
                nc.tensor.matmul(bank[:, q, :], d_t[i][:, q, :], ident[:], start=True, stop=False, is_transpose=True)
                nc.tensor.matmul(bank[:, q, :], bt_t[i][:, q, :], ident[:], start=False, stop=True, is_transpose=True)
            bbank[i] = bank[:].rearrange("p q r -> p (q r)")

        def OT(i):
            bank = ptr.tile([P, 4, P], F32, name="tr2", tag="tr")
            for t in range(4):
                nc.tensor.transpose(bank[:, t, :], o_t[i][:, t : R : 4], ident[:])
            tr["o", i] = bank

        def OC(i):
            bank = tr["o", i]
            if i // 2 not in oi:
                oi[i // 2] = work.tile([P, 2 * P, 4], BF16, name="oi", tag="gi", bufs=5, align_bytes=64)
            nc.scalar.copy(
                out=oi[i // 2][:, P * (i % 2) : P * (i % 2 + 1), :], in_=bank[:].rearrange("p t d -> p d t")
            )

        def QO(i0, n):
            cols = slice(P * i0, P * (i0 + n))
            first = i0 % 2
            nc.vector.quantize_mx(
                out=o_codes[:, cols].bitcast(E4M3),
                scales=o_scales[:, cols],
                in_=oi[i0 // 2][:, P * first : P * (first + n), :].rearrange("p d t -> p (d t)"),
            )
            nc.sync.dma_start(
                out=out_1[0].rearrange("p m t -> p (m t)").bitcast(I32)[:, cols], in_=o_codes[:, cols].bitcast(I32)
            )

        def SC(lo, hi):
            for q in range(4):
                nc.scalar.dma_start(
                    out=out_2[0, 4 * q : 4 * q + 4, lo:hi].bitcast(I32),
                    in_=o_scales[32 * q : 32 * q + 4, lo:hi].bitcast(I32),
                )

        LAM()
        T(0, 0)
        T(0, 2)
        GC(0, 0)
        GC(0, 2)
        T(0, 1)
        T(0, 3)
        GC(0, 1)
        QG(0, 0)
        GC(0, 3)
        T(1, 0)
        T(1, 1)
        QG(0, 1)
        T(1, 2)
        LC()
        M(0, 0)
        M(0, 3)
        M(0, 2)
        M(0, 1)
        GC(1, 0)
        T(1, 3)
        T(2, 0)
        L(0, 0)
        GC(1, 1)
        QG(1, 0)
        GC(1, 2)
        T(2, 2)
        XI(0, 1, "S")
        L(0, 2)
        XI(0, 0, "S")
        GC(1, 3)
        L(0, 1)
        GC(2, 0)
        T(2, 1)
        L(0, 3)
        GC(2, 2)
        QG(1, 1)
        GC(2, 1)
        XI(1, 1, "S")
        QU(0)
        T(2, 3)
        M(1, 0)
        M(1, 3)
        M(1, 2)
        GC(2, 3)
        QX(0, 0)
        QG(2, 0)
        M(1, 1)
        L(1, 0)
        XI(2, 0, "S")
        L(1, 3)
        QG(2, 1)
        T(3, 1)
        T(3, 0)
        XI(1, 0, "S")
        L(1, 1)
        T(3, 2)
        L(1, 2)
        T(3, 3)
        M(2, 0)
        QX(2, 0)
        M(2, 2)
        GC(3, 2)
        QX(0, 1)
        GC(3, 0)
        QX(1, 1)
        QX(1, 0)
        QU(1)
        L(2, 0)
        GC(3, 3)
        QG(3, 1)
        M(2, 3)
        GC(3, 1)
        M(2, 1)
        XI(3, 1, "S")
        QG(3, 0)
        NEG(1)
        NEG(4)
        M(3, 0)
        L(2, 3)
        L(2, 2)
        L(3, 0)
        L(2, 1)
        M(3, 1)
        L(3, 1)
        M(3, 3)
        M(3, 2)
        L(3, 3)
        QX(3, 1)
        L(3, 2)
        XI(3, 0, "S")
        N(0, 0)
        XI(2, 1, "S")
        QU(2)
        QX(2, 1)
        N(2, 0)
        BT(1)
        QU(3)
        XI(0, 3, "S")
        N(0, 1)
        QX(0, 3)
        N(3, 0)
        N(1, 0)
        XI(1, 2, "S")
        N(2, 1)
        N(2, 2)
        N(3, 1)
        XI(2, 3, "S")
        N(3, 2)
        N(3, 3)
        QX(3, 0)
        XI(0, 2, "S")
        N(0, 2)
        QX(1, 2)
        N(2, 3)
        PR(3)
        N(1, 1)
        PR(2)
        N(0, 3)
        PR(0)
        N(1, 2)
        BT(4)
        S1(3)
        QX(2, 3)
        QX(0, 2)
        S1(2)
        N(1, 3)
        PR(1)
        XI(2, 2, "S")
        S1(0)
        DF(3)
        DF(2)
        S2(2)
        N(7, 0)
        S2(3)
        S1(1)
        A(3)
        XI(1, 3, "S")
        A(2)
        N(6, 0)
        QX(2, 2)
        B(2)
        DF(0)
        XI(3, 2, "S")
        N(5, 0)
        N(5, 1)
        B(3)
        N(5, 2)
        O(2)
        O(3)
        N(4, 0)
        N(4, 1)
        DT(1)
        S2(0)
        XI(3, 3, "S")
        QX(1, 3)
        OT(2)
        A(1)
        N(7, 1)
        N(7, 2)
        A(0)
        BC(1)
        B(0)
        N(4, 2)
        E2(1)
        N(6, 1)
        QX(3, 2)
        N(6, 2)
        N(5, 3)
        O(0)
        N(4, 3)
        QX(3, 3)
        N(7, 3)
        N(6, 3)
        BP(1)
        PR(5)
        PR(4)
        BC(4)
        PR(7)
        PR(6)
        S1(5)
        O(1)
        S1(4)
        DT(4)
        S1(7)
        OC(2)
        E2(4)
        DF(5)
        DF(7)
        OT(3)
        A(4)
        OT(1)
        S1(6)
        S2(7)
        A(7)
        A(5)
        OC(3)
        S2(5)
        DF(6)
        S2(6)
        B(5)
        BP(4)
        OT(0)
        O(4)
        OC(0)
        B(7)
        A(6)
        OC(1)
        O(5)
        OT(4)
        OT(5)
        OC(4)
        O(7)
        OT(7)
        B(6)
        O(6)
        OC(7)
        QO(7, 1)
        OC(5)
        QO(2, 2)
        OT(6)
        QO(0, 2)
        OC(6)
        QO(4, 2)
        QO(6, 1)
        SC(0, D)
